import numpy as np
import ml_dtypes


def mxq(x, axis, fmt="e4m3"):
    dtype, down = {"e4m3": (ml_dtypes.float8_e4m3fn, 7), "e5m2": (ml_dtypes.float8_e5m2, 14)}[fmt]
    v = np.moveaxis(np.asarray(x, np.float32).astype(ml_dtypes.bfloat16).astype(np.float64), axis, -1)
    blocks = v.reshape(v.shape[:-1] + (-1, 32))
    amax = np.abs(blocks).max(-1, keepdims=True)
    byte = np.maximum(np.where(amax > 0, np.frexp(amax)[1] - 1 + 127, 0) - down, 1)
    scale = np.exp2(byte - 127.0)
    codes = (blocks / scale).astype(np.float32).astype(dtype).astype(np.float64)
    return np.moveaxis((codes * scale).reshape(v.shape), -1, axis)


WIDE = False


def mx_kscale(k):
    if not WIDE:
        return np.ones(k)
    levels = np.array([10, -10, 5, -5, 0])
    if k % 512:
        return np.exp2(np.random.permutation(np.resize(levels, k // 32))).repeat(32)
    a = np.empty((k // 512, 16))
    for p in range(k // 512):
        a[p, :8] = np.random.permutation(np.resize(levels, 8))
        for g in range(8):
            far = levels[np.abs(levels - a[p, g]) >= 10]
            a[p, g + 8] = far[np.random.randint(len(far))]
    return np.exp2(a.ravel()).repeat(32)


def f64(x):
    return np.asarray(x).astype(np.float64)


def striped(idx):
    return np.tile(idx.reshape(-1, 16).T, (8, 1)).astype(np.uint16)


def unstriped(offs):
    return offs[:16].T.reshape(-1).astype(np.int64)


E2M1 = np.array([0.0, 0.5, 1.0, 1.5, 2.0, 3.0, 4.0, 6.0, -0.0, -0.5, -1.0, -1.5, -2.0, -3.0, -4.0, -6.0])


def pack_weight(w, fmt):
    k, n = w.shape
    w = f64(np.asarray(w, np.float32).astype(ml_dtypes.bfloat16)).reshape(k // 32, 32, n)
    amax = np.abs(w).max(1)
    if fmt == "e4m3":
        byte = np.frexp(amax)[1] - 1 + 127 - 7
    else:
        mant, ex = np.frexp(amax / 6.0)
        byte = np.where(mant > 0.5, ex, ex - 1) + 127
    byte = np.clip(np.where(amax > 0, byte, 1), 1, 254)
    scaled = (w * np.exp2(127.0 - byte)[:, None, :]).reshape(k, n).astype(np.float32)
    by_word = np.ascontiguousarray(scaled.reshape(k // 512, 128, 4, n).transpose(0, 1, 3, 2))
    if fmt == "e4m3":
        words = by_word.astype(ml_dtypes.float8_e4m3fn).view(np.uint8)
    else:
        c = by_word.astype(ml_dtypes.float4_e2m1fn).view(np.uint8) & 0xF
        words = (c[..., 0::2] | (c[..., 1::2] << 4)).reshape(k // 512, 128, 2 * n)
    return np.ascontiguousarray(words), np.ascontiguousarray(byte.astype(np.uint8).reshape(k // 512, 16, n))


def unpack_weight(words, scales, fmt):
    g, _, n = scales.shape
    words = np.ascontiguousarray(words).reshape(g, 128, n, -1)
    if fmt == "e4m3":
        vals = words.view(ml_dtypes.float8_e4m3fn).astype(np.float64)
    else:
        nib = np.empty((g, 128, n, 4), np.uint8)
        nib[..., 0::2] = words & 0xF
        nib[..., 1::2] = words >> 4
        vals = E2M1[nib]
    vals = vals * np.repeat(np.exp2(scales.astype(np.float64) - 127.0), 8, axis=1)[..., None]
    return vals.transpose(0, 1, 3, 2).reshape(g * 512, n)


def gelu(v):
    return 0.5 * v * (1.0 + np.tanh(np.sqrt(2.0 / np.pi) * (v + 0.044715 * v**3)))


def striped8(idx):
    return np.concatenate([v.reshape(-1, 16).T for v in idx]).astype(np.uint16)


def unstriped8(offs):
    return np.stack([offs[16 * g:16 * g + 16].T.reshape(-1) for g in range(8)]).astype(np.int64)


def put_heads(h, wgs, idx8, t2):
    r = np.arange(h.shape[0])
    page = np.zeros((h.shape[0], t2))
    page[r[:, None], idx8[r % 512 // 64]] = wgs[r // 4 % 128] * h
    return page


K, H, N, T, S, T2, P = 1024, 512, 256, 2048, 1024, 2048, 1024

def setup_inputs():
    n = np.random.standard_normal
    s = mx_kscale(K)[:, None]
    u = mx_kscale(H)[:, None]
    tab_words, tab_scales = pack_weight(n((K, T)) * s, "e4m3")
    w2_words, w2_scales = pack_weight(n((K, H)) / np.sqrt(K) / s * u.T, "e2m1")
    w4_words, w4_scales = pack_weight(0.8 * n((H, N)) / np.sqrt(H) / u, "e2m1")
    w5_words, w5_scales = pack_weight(n((K, N)) / np.sqrt(K) / s, "e4m3")
    return {
        "tab_words": tab_words, "tab_scales": tab_scales,
        "offs": striped(np.random.permutation(T)[:S]),
        "offs2": striped8(np.stack([np.random.permutation(T2)[:S] for _ in range(8)])),
        "offs3": striped(np.random.permutation(T2)[:P]),
        "w1": (n((K, H)) / np.sqrt(K) / s * u.T).astype(np.float32),
        "w2_words": w2_words, "w2_scales": w2_scales,
        "wgs": np.repeat(np.random.uniform(0.5, 2.0, (8, S)), 16, axis=0).astype(np.float32),
        "noise": (n((H, P)) * u).astype(np.float32),
        "w3": (0.8 * n((H, N)) / np.sqrt(H) / u).astype(np.float32),
        "w4_words": w4_words, "w4_scales": w4_scales,
        "w5_words": w5_words, "w5_scales": w5_scales,
    }

def reference(tab_words, tab_scales, offs, offs2, offs3, w1, w2_words, w2_scales, wgs, noise, w3, w4_words, w4_scales, w5_words, w5_scales):
    v = unpack_weight(tab_words, tab_scales, "e4m3")[:, unstriped(offs)]
    w2 = unpack_weight(w2_words, w2_scales, "e2m1")
    w4 = unpack_weight(w4_words, w4_scales, "e2m1")
    w5 = unpack_weight(w5_words, w5_scales, "e4m3")
    even = mxq(f64(w1), 0, "e4m3").T @ v
    odd = w2.T @ v
    h = np.sqrt(np.square(even) + np.square(odd))
    page = put_heads(h, f64(wgs), unstriped8(offs2), T2)
    x = page[:, unstriped(offs3)]
    d = mxq(x + f64(noise), 0, "e4m3")
    y1 = mxq(f64(w3), 0, "e4m3").T @ d
    y2 = w4.T @ d
    skip = w5.T @ v
    return y1 * y2 + skip

@@ -1,0 +1,251 @@
+from contextlib import ExitStack
+
+import concourse.mybir as mybir
+from concourse.masks import make_identity
+
+K, H, N, T, S, T2 = 1024, 512, 256, 2048, 1024, 2048
+FLOPS = 2 * K * H * S * 2 + 2 * H * N * S * 2 + 2 * K * N * S
+
+F32 = mybir.dt.float32
+BF16 = mybir.dt.bfloat16
+I32 = mybir.dt.int32
+U32 = mybir.dt.uint32
+U16 = mybir.dt.uint16
+U8 = mybir.dt.uint8
+FP8X4 = mybir.dt.float8_e4m3fn_x4
+FP4X4 = mybir.dt.float4_e2m1fn_x4
+ACT = mybir.ActivationFunctionType
+ALU = mybir.AluOpType
+
+P = 128
+PACK = 4
+K_PASS = P * PACK
+PASSES = K // K_PASS
+BANK = 512
+LOOKUP_CUTS = (0, 256, 512, 1024)
+PUT_CUTS = (0, 128, 256, 512, 768, 1024)
+FETCH_CUTS = (0, 256, 512, 768, 896, 1024)
+
+
+def spans(cuts):
+    return list(zip(cuts[:-1], cuts[1:]))
+
+
+def entries(offsets, lo, hi):
+    return offsets[:, lo // 16 : hi // 16]
+
+
+def load_scale_rows(queue, plane, scales):
+    for q in range(4):
+        queue.dma_start(
+            out=plane[32 * q : 32 * q + 4].bitcast(I32),
+            in_=scales[:, 4 * q : 4 * q + 4, :].rearrange("a r c -> r a c").bitcast(I32),
+        )
+
+
+def interleave(nc, grouped, rows):
+    nc.scalar.copy(
+        out=grouped.rearrange("p (c e) i -> p c i e", e=4),
+        in_=rows.rearrange("p i (c e) -> p c i e", e=4),
+    )
+
+
+def quantize(nc, codes, scales, grouped):
+    nc.vector.quantize_mx(out=codes.bitcast(FP8X4), scales=scales, in_=grouped.rearrange("p c i -> p (c i)"))
+
+
+def tile_list_sonobuoy_cue_features_kernel(
+    tc, tab_words, tab_scales, offs, offs2, offs3, w1, w2_words, w2_scales, wgs, noise, w3,
+    w4_words, w4_scales, w5_words, w5_scales, out,
+):
+    nc = tc.nc
+    with ExitStack() as ctx:
+        keep = ctx.enter_context(tc.tile_pool(name="keep", bufs=1))
+        ring = ctx.enter_context(tc.tile_pool(name="ring", bufs=2))
+        psum = ctx.enter_context(tc.psum_pool(name="psum", bufs=2))
+
+        def held(name, shape, dtype, after=None):
+            return keep.tile(shape, dtype, name=name, tag=after or name, align_bytes=64)
+
+        lookup_list = held("lookup_list", [P, S // 16], U16)
+        put_list = held("put_list", [P, S // 16], U16)
+        fetch_list = held("fetch_list", [P, S // 16], U16)
+
+        tab_sc = held("tab_sc", [P, PASSES, T], U8)
+        w2_sc = held("w2_sc", [P, PASSES, H], U8)
+        w5_sc = held("w5_sc", [P, PASSES, N], U8)
+        w4_sc = held("w4_sc", [P, 1, N], U8)
+        nc.gpsimd.memset(tab_sc[:].bitcast(I32), 0)
+        nc.gpsimd.memset(w2_sc[:].bitcast(I32), 0)
+        load_scale_rows(nc.gpsimd, w2_sc, w2_scales)
+        identity = held("identity", [P, P], F32)
+        make_identity(nc, identity[:])
+        pages = [held("page%d" % i, [P, T2], F32) for i in range(PACK)]
+        for page in pages:
+            for half in range(2):
+                nc.gpsimd.memset(page[:, half * T2 // 2 : (half + 1) * T2 // 2], 0.0)
+        for plane in (w5_sc, w4_sc):
+            nc.gpsimd.memset(plane[:].bitcast(I32), 0)
+
+        tab_w = [held("tab_w%d" % a, [P, T], I32) for a in range(PASSES)]
+        w1_raw = [held("w1_raw%d" % a, [P, PACK, H], F32) for a in range(PASSES)]
+        w2_w = held("w2_w", [P, PASSES, 2 * H], U8)
+
+        def load_tab(a):
+            nc.sync.dma_start(out=tab_w[a][:], in_=tab_words[a].rearrange("p t i -> p (t i)").bitcast(I32))
+
+        def load_w1(a):
+            rows = w1[a * K_PASS : (a + 1) * K_PASS, :]
+            nc.sync.dma_start(out=w1_raw[a][:], in_=rows.rearrange("(p i) r -> p i r", i=PACK))
+
+        load_scale_rows(nc.scalar, tab_sc, tab_scales)
+        nc.sync.dma_start(lookup_list[:], offs)
+        nc.sync.dma_start(put_list[:], offs2)
+        nc.sync.dma_start(fetch_list[:], offs3)
+        load_tab(0)
+        load_w1(0)
+        load_w1(1)
+        nc.sync.dma_start(out=w2_w[:].bitcast(I32), in_=w2_words.rearrange("a p c -> p a c").bitcast(I32))
+        load_tab(1)
+
+        w1_codes = [held("w1_codes%d" % a, [P, H], U32) for a in range(PASSES)]
+        w1_sc = [held("w1_sc%d" % a, [P, H], U8) for a in range(PASSES)]
+        w1_bf = [held("w1_bf%d" % a, [P, H, PACK], BF16) for a in range(PASSES)]
+        v_w = [[held("v_w%d_%d" % (a, lo), [P, hi - lo], U32) for lo, hi in spans(LOOKUP_CUTS)] for a in range(PASSES)]
+        v_sc = [[held("v_sc%d_%d" % (a, lo), [P, hi - lo], U8) for lo, hi in spans(LOOKUP_CUTS)] for a in range(PASSES)]
+
+        def looked_up(a, j0, width):
+            part = max(n for n, (lo, hi) in enumerate(spans(LOOKUP_CUTS)) if lo <= j0)
+            cols = slice(j0 - LOOKUP_CUTS[part], j0 - LOOKUP_CUTS[part] + width)
+            return v_w[a][part][:, cols].bitcast(FP8X4), v_sc[a][part][:, cols]
+
+        def look_up_words(a, part):
+            lo, hi = spans(LOOKUP_CUTS)[part]
+            nc.vector.tensor_copy(v_w[a][part][:], tab_w[a][:].bitcast(U32).indirect(entries(lookup_list, lo, hi)))
+
+        def look_up_scales(part):
+            lo, hi = spans(LOOKUP_CUTS)[part]
+            for a in range(PASSES):
+                nc.vector.tensor_copy(v_sc[a][part][:], tab_sc[:, a, :].indirect(entries(lookup_list, lo, hi)))
+
+        for a in range(PASSES):
+            interleave(nc, w1_bf[a][:], w1_raw[a][:])
+        look_up_scales(0)
+        quantize(nc, w1_codes[0][:], w1_sc[0][:], w1_bf[0][:])
+        look_up_scales(1)
+        look_up_words(0, 0)
+        quantize(nc, w1_codes[1][:], w1_sc[1][:], w1_bf[1][:])
+        look_up_words(0, 1)
+        look_up_words(0, 2)
+        look_up_words(1, 0)
+        look_up_words(1, 1)
+        look_up_scales(2)
+        look_up_words(1, 2)
+
+        wgs_sb = held("wgs_sb", [P, S], F32, after="w1_raw0")
+        w3_raw = held("w3_raw", [P, PACK, N], F32, after="w1_raw1")
+        w5_w = held("w5_w", [P, PASSES, N], I32, after="w1_bf0")
+        w4_w = held("w4_w", [P, 2 * N], U8, after="w1_bf1")
+        nc.sync.dma_start(out=wgs_sb[:], in_=wgs)
+        nc.sync.dma_start(out=w5_w[:], in_=w5_words.rearrange("a p c i -> p a (c i)").bitcast(I32))
+        nc.sync.dma_start(out=w3_raw[:], in_=w3.rearrange("(p i) n -> p i n", i=PACK))
+        nc.sync.dma_start(out=w4_w[:].bitcast(I32), in_=w4_words[0].bitcast(I32))
+        load_scale_rows(nc.sync, w5_sc, w5_scales)
+        load_scale_rows(nc.sync, w4_sc, w4_scales)
+        noise_rows = noise.rearrange("(p i) j -> p i j", i=PACK)
+        noise_sb = []
+        for a in range(PASSES):
+            pair = held("noise%d" % a, [P, 2, S], F32, after="tab_w%d" % a)
+            nc.sync.dma_start(out=pair[:], in_=noise_rows[:, 2 * a : 2 * a + 2, :])
+            noise_sb.extend([pair[:, 0, :], pair[:, 1, :]])
+
+        for lo, hi in spans(PUT_CUTS):
+            h = held("h%d" % lo, [P, PACK, hi - lo], F32)
+            for j0 in range(lo, hi, P):
+                even = psum.tile([P, H], F32, name="even", bufs=1)
+                odd = psum.tile([P, H], F32, name="odd", bufs=1)
+                for a in range(PASSES):
+                    nc.tensor.matmul_mx(
+                        out=even[:], lhsT=looked_up(a, j0, P)[0], lhsT_scale=looked_up(a, j0, P)[1],
+                        rhs=w1_codes[a][:].bitcast(FP8X4), rhs_scale=w1_sc[a][:],
+                        start=(a == 0), stop=(a == PASSES - 1),
+                    )
+                for a in range(PASSES):
+                    nc.tensor.matmul_mx(
+                        out=odd[:], lhsT=looked_up(a, j0, P)[0], lhsT_scale=looked_up(a, j0, P)[1],
+                        rhs=w2_w[:, a, :].bitcast(FP4X4), rhs_scale=w2_sc[:, a, :],
+                        start=(a == 0), stop=(a == PASSES - 1),
+                    )
+                even_sq = ring.tile([P, PACK, P], F32, name="even_sq")
+                odd_sq = ring.tile([P, PACK, P], F32, name="odd_sq")
+                nc.scalar.activation(even_sq[:], even[:].rearrange("j (p i) -> j i p", i=PACK), ACT.Square)
+                nc.scalar.activation(odd_sq[:], odd[:].rearrange("j (p i) -> j i p", i=PACK), ACT.Square)
+                power = psum.tile([P, PACK, P], F32, name="power")
+                for i in range(PACK):
+                    nc.tensor.matmul(power[:, i, :], lhsT=even_sq[:, i, :], rhs=identity[:],
+                                     start=True, stop=False, is_transpose=True)
+                    nc.tensor.matmul(power[:, i, :], lhsT=odd_sq[:, i, :], rhs=identity[:],
+                                     start=False, stop=True, is_transpose=True)
+                nc.scalar.activation(h[:, :, j0 - lo : j0 - lo + P], power[:], ACT.Sqrt)
+            for i in range(PACK):
+                nc.vector.tensor_tensor(
+                    pages[i][:].indirect(entries(put_list, lo, hi)), h[:, i, :], wgs_sb[:, lo:hi], ALU.mult
+                )
+
+        skip = held("skip", [P, N // P, S], F32)
+        for b in range(N // P):
+            rows = slice(b * P, (b + 1) * P)
+            for j0 in range(0, S, BANK):
+                acc = psum.tile([P, BANK], F32, name="power")
+                for lo, hi in spans(LOOKUP_CUTS):
+                    if j0 <= lo < j0 + BANK:
+                        for a in range(PASSES):
+                            codes, scales = looked_up(a, lo, hi - lo)
+                            nc.tensor.matmul_mx(
+                                out=acc[:, lo - j0 : hi - j0], lhsT=w5_w[:, a, rows].bitcast(FP8X4),
+                                lhsT_scale=w5_sc[:, a, rows], rhs=codes, rhs_scale=scales,
+                                start=(a == 0), stop=(a == PASSES - 1),
+                            )
+                nc.scalar.copy(out=skip[:, b, j0 : j0 + BANK], in_=acc[:])
+
+        w3_codes = held("w3_codes", [P, N], U32)
+        w3_sc = held("w3_sc", [P, N], U8)
+        w3_bf = held("w3_bf", [P, N, PACK], BF16)
+        interleave(nc, w3_bf[:], w3_raw[:])
+        quantize(nc, w3_codes[:], w3_sc[:], w3_bf[:])
+
+        out_rows = out.rearrange("(b p) j -> p b j", p=P)
+        for lo, hi in spans(FETCH_CUTS):
+            width = hi - lo
+            d = ring.tile([P, PACK, width], F32, name="d")
+            for i in range(PACK):
+                nc.vector.tensor_tensor(
+                    d[:, i, :], pages[i][:].indirect(entries(fetch_list, lo, hi)), noise_sb[i][:, lo:hi], ALU.add
+                )
+            d_bf = ring.tile([P, width, PACK], BF16, name="d_bf", align_bytes=64)
+            interleave(nc, d_bf[:], d[:])
+            d_codes = ring.tile([P, width], U32, name="d_codes", align_bytes=64)
+            d_sc = ring.tile([P, width], U8, name="d_sc", align_bytes=64)
+            quantize(nc, d_codes[:], d_sc[:], d_bf[:])
+            y1 = psum.tile([P, N // P, width], F32, name="y1")
+            y2 = psum.tile([P, N // P, width], F32, name="y2")
+            for b in range(N // P):
+                rows = slice(b * P, (b + 1) * P)
+                nc.tensor.matmul_mx(
+                    out=y1[:, b, :], lhsT=w3_codes[:, rows].bitcast(FP8X4), lhsT_scale=w3_sc[:, rows],
+                    rhs=d_codes[:].bitcast(FP8X4), rhs_scale=d_sc[:], start=True, stop=True,
+                )
+            for b in range(N // P):
+                rows = slice(b * P, (b + 1) * P)
+                nc.tensor.matmul_mx(
+                    out=y2[:, b, :], lhsT=w4_w[:, 2 * b * P : 2 * (b + 1) * P].bitcast(FP4X4),
+                    lhsT_scale=w4_sc[:, 0, rows],
+                    rhs=d_codes[:].bitcast(FP8X4), rhs_scale=d_sc[:], start=True, stop=True,
+                )
+            y1_sb = ring.tile([P, N // P, width], F32, name="y1_sb")
+            nc.scalar.copy(out=y1_sb[:], in_=y1[:])
+            prod = ring.tile([P, N // P, width], F32, name="prod")
+            nc.vector.tensor_tensor(prod[:], y2[:], y1_sb[:], ALU.mult)
+            result = ring.tile([P, N // P, width], F32, name="result")
+            nc.vector.tensor_tensor(result[:], prod[:], skip[:, :, lo:hi], ALU.add)
+            nc.sync.dma_start(out=out_rows[:, :, lo:hi], in_=result[:])

@@ -23,7 +23,7 @@ K_PASS = P * PACK
 PASSES = K // K_PASS
 BANK = 512
 LOOKUP_CUTS = (0, 256, 512, 1024)
-PUT_CUTS = (0, 128, 256, 512, 768, 1024)
+PUT_CUTS = (0, 128, 256, 384, 512, 768, 1024)
 FETCH_CUTS = (0, 256, 512, 768, 896, 1024)
 
 
@@ -77,15 +77,17 @@ def tile_list_sonobuoy_cue_features_kernel(
         w4_sc = held("w4_sc", [P, 1, N], U8)
         nc.gpsimd.memset(tab_sc[:].bitcast(I32), 0)
         nc.gpsimd.memset(w2_sc[:].bitcast(I32), 0)
-        load_scale_rows(nc.gpsimd, w2_sc, w2_scales)
         identity = held("identity", [P, P], F32)
         make_identity(nc, identity[:])
+        load_scale_rows(nc.gpsimd, w2_sc, w2_scales)
         pages = [held("page%d" % i, [P, T2], F32) for i in range(PACK)]
         for page in pages:
-            for half in range(2):
-                nc.gpsimd.memset(page[:, half * T2 // 2 : (half + 1) * T2 // 2], 0.0)
+            nc.vector.memset(page[:], 0.0)
         for plane in (w5_sc, w4_sc):
             nc.gpsimd.memset(plane[:].bitcast(I32), 0)
+
+        warm = held("warm", [P, 1], F32)
+        nc.scalar.activation(warm[:], identity[:, 0:1], ACT.Sqrt, bias=1.0)
 
         tab_w = [held("tab_w%d" % a, [P, T], I32) for a in range(PASSES)]
         w1_raw = [held("w1_raw%d" % a, [P, PACK, H], F32) for a in range(PASSES)]
@@ -102,8 +104,8 @@ def tile_list_sonobuoy_cue_features_kernel(
         nc.sync.dma_start(lookup_list[:], offs)
         nc.sync.dma_start(put_list[:], offs2)
         nc.sync.dma_start(fetch_list[:], offs3)
-        load_tab(0)
         load_w1(0)
+        load_tab(0)
         load_w1(1)
         nc.sync.dma_start(out=w2_w[:].bitcast(I32), in_=w2_words.rearrange("a p c -> p a c").bitcast(I32))
         load_tab(1)
@@ -131,12 +133,11 @@ def tile_list_sonobuoy_cue_features_kernel(
         for a in range(PASSES):
             interleave(nc, w1_bf[a][:], w1_raw[a][:])
         look_up_scales(0)
-        quantize(nc, w1_codes[0][:], w1_sc[0][:], w1_bf[0][:])
         look_up_scales(1)
-        look_up_words(0, 0)
+        quantize(nc, w1_codes[0][:], w1_sc[0][:], w1_bf[0][:])
+        for part in range(3):
+            look_up_words(0, part)
         quantize(nc, w1_codes[1][:], w1_sc[1][:], w1_bf[1][:])
-        look_up_words(0, 1)
-        look_up_words(0, 2)
         look_up_words(1, 0)
         look_up_words(1, 1)
         look_up_scales(2)
@@ -162,8 +163,8 @@ def tile_list_sonobuoy_cue_features_kernel(
         for lo, hi in spans(PUT_CUTS):
             h = held("h%d" % lo, [P, PACK, hi - lo], F32)
             for j0 in range(lo, hi, P):
-                even = psum.tile([P, H], F32, name="even", bufs=1)
-                odd = psum.tile([P, H], F32, name="odd", bufs=1)
+                even = psum.tile([P, H], F32, name="even")
+                odd = psum.tile([P, H], F32, name="odd")
                 for a in range(PASSES):
                     nc.tensor.matmul_mx(
                         out=even[:], lhsT=looked_up(a, j0, P)[0], lhsT_scale=looked_up(a, j0, P)[1],
@@ -183,30 +184,28 @@ def tile_list_sonobuoy_cue_features_kernel(
                 power = psum.tile([P, PACK, P], F32, name="power")
                 for i in range(PACK):
                     nc.tensor.matmul(power[:, i, :], lhsT=even_sq[:, i, :], rhs=identity[:],
-                                     start=True, stop=False, is_transpose=True)
+                                     start=(i == 0), stop=False, is_transpose=True)
+                for i in range(PACK):
                     nc.tensor.matmul(power[:, i, :], lhsT=odd_sq[:, i, :], rhs=identity[:],
-                                     start=False, stop=True, is_transpose=True)
+                                     start=False, stop=(i == PACK - 1), is_transpose=True)
                 nc.scalar.activation(h[:, :, j0 - lo : j0 - lo + P], power[:], ACT.Sqrt)
             for i in range(PACK):
                 nc.vector.tensor_tensor(
                     pages[i][:].indirect(entries(put_list, lo, hi)), h[:, i, :], wgs_sb[:, lo:hi], ALU.mult
                 )
 
-        skip = held("skip", [P, N // P, S], F32)
-        for b in range(N // P):
-            rows = slice(b * P, (b + 1) * P)
-            for j0 in range(0, S, BANK):
-                acc = psum.tile([P, BANK], F32, name="power")
-                for lo, hi in spans(LOOKUP_CUTS):
-                    if j0 <= lo < j0 + BANK:
-                        for a in range(PASSES):
-                            codes, scales = looked_up(a, lo, hi - lo)
-                            nc.tensor.matmul_mx(
-                                out=acc[:, lo - j0 : hi - j0], lhsT=w5_w[:, a, rows].bitcast(FP8X4),
-                                lhsT_scale=w5_sc[:, a, rows], rhs=codes, rhs_scale=scales,
-                                start=(a == 0), stop=(a == PASSES - 1),
-                            )
-                nc.scalar.copy(out=skip[:, b, j0 : j0 + BANK], in_=acc[:])
+        skip_t = held("skip_t", [P, S // P, N], F32)
+        for pair in range(S // P // 2):
+            acc = psum.tile([P, 2, N], F32, name="power")
+            for u in range(2):
+                for a in range(PASSES):
+                    codes, scales = looked_up(a, (2 * pair + u) * P, P)
+                    nc.tensor.matmul_mx(
+                        out=acc[:, u, :], lhsT=codes, lhsT_scale=scales,
+                        rhs=w5_w[:, a, :].bitcast(FP8X4), rhs_scale=w5_sc[:, a, :],
+                        start=(a == 0), stop=(a == PASSES - 1),
+                    )
+            nc.scalar.copy(out=skip_t[:, 2 * pair : 2 * pair + 2, :], in_=acc[:])
 
         w3_codes = held("w3_codes", [P, N], U32)
         w3_sc = held("w3_sc", [P, N], U8)
@@ -227,25 +226,33 @@ def tile_list_sonobuoy_cue_features_kernel(
             d_codes = ring.tile([P, width], U32, name="d_codes", align_bytes=64)
             d_sc = ring.tile([P, width], U8, name="d_sc", align_bytes=64)
             quantize(nc, d_codes[:], d_sc[:], d_bf[:])
-            y1 = psum.tile([P, N // P, width], F32, name="y1")
-            y2 = psum.tile([P, N // P, width], F32, name="y2")
-            for b in range(N // P):
-                rows = slice(b * P, (b + 1) * P)
+            blocks = width // P
+            y1 = psum.tile([P, blocks, N], F32, name="even")
+            y2 = psum.tile([P, blocks, N], F32, name="odd")
+            for u in range(blocks):
+                cols = slice(u * P, (u + 1) * P)
                 nc.tensor.matmul_mx(
-                    out=y1[:, b, :], lhsT=w3_codes[:, rows].bitcast(FP8X4), lhsT_scale=w3_sc[:, rows],
-                    rhs=d_codes[:].bitcast(FP8X4), rhs_scale=d_sc[:], start=True, stop=True,
+                    out=y1[:, u, :], lhsT=d_codes[:, cols].bitcast(FP8X4), lhsT_scale=d_sc[:, cols],
+                    rhs=w3_codes[:].bitcast(FP8X4), rhs_scale=w3_sc[:], start=True, stop=True,
                 )
-            for b in range(N // P):
-                rows = slice(b * P, (b + 1) * P)
+            for u in range(blocks):
+                cols = slice(u * P, (u + 1) * P)
                 nc.tensor.matmul_mx(
-                    out=y2[:, b, :], lhsT=w4_w[:, 2 * b * P : 2 * (b + 1) * P].bitcast(FP4X4),
-                    lhsT_scale=w4_sc[:, 0, rows],
-                    rhs=d_codes[:].bitcast(FP8X4), rhs_scale=d_sc[:], start=True, stop=True,
+                    out=y2[:, u, :], lhsT=d_codes[:, cols].bitcast(FP8X4), lhsT_scale=d_sc[:, cols],
+                    rhs=w4_w[:].bitcast(FP4X4), rhs_scale=w4_sc[:, 0, :], start=True, stop=True,
                 )
-            y1_sb = ring.tile([P, N // P, width], F32, name="y1_sb")
+            y1_sb = ring.tile([P, blocks, N], F32, name="y1_sb")
             nc.scalar.copy(out=y1_sb[:], in_=y1[:])
-            prod = ring.tile([P, N // P, width], F32, name="prod")
+            prod = ring.tile([P, blocks, N], F32, name="prod")
             nc.vector.tensor_tensor(prod[:], y2[:], y1_sb[:], ALU.mult)
+            total = psum.tile([P, N // P, width], F32, name="power")
+            squares = [(b, u) for u in range(blocks) for b in range(N // P)]
+            for n, (b, u) in enumerate(squares):
+                nc.tensor.matmul(total[:, b, u * P : (u + 1) * P], lhsT=skip_t[:, lo // P + u, b * P : (b + 1) * P],
+                                 rhs=identity[:], start=(n == 0), stop=False, is_transpose=True)
+            for n, (b, u) in enumerate(squares):
+                nc.tensor.matmul(total[:, b, u * P : (u + 1) * P], lhsT=prod[:, u, b * P : (b + 1) * P],
+                                 rhs=identity[:], start=False, stop=(n == len(squares) - 1), is_transpose=True)
             result = ring.tile([P, N // P, width], F32, name="result")
-            nc.vector.tensor_tensor(result[:], prod[:], skip[:, :, lo:hi], ALU.add)
+            nc.scalar.copy(out=result[:], in_=total[:])
             nc.sync.dma_start(out=out_rows[:, :, lo:hi], in_=result[:])

@@ -1,7 +1,6 @@
 from contextlib import ExitStack
 
 import concourse.mybir as mybir
-from concourse.masks import make_identity
 
 K, H, N, T, S, T2 = 1024, 512, 256, 2048, 1024, 2048
 FLOPS = 2 * K * H * S * 2 + 2 * H * N * S * 2 + 2 * K * N * S
@@ -21,9 +20,9 @@ P = 128
 PACK = 4
 K_PASS = P * PACK
 PASSES = K // K_PASS
-BANK = 512
-LOOKUP_CUTS = (0, 256, 512, 1024)
-PUT_CUTS = (0, 128, 256, 384, 512, 768, 1024)
+TURNED = 768
+FIRST_LOOKUP = 256
+PUT_CUTS = (0, 128, 256, 512, 768, 1024)
 FETCH_CUTS = (0, 256, 512, 768, 896, 1024)
 
 
@@ -61,11 +60,18 @@ def tile_list_sonobuoy_cue_features_kernel(
     nc = tc.nc
     with ExitStack() as ctx:
         keep = ctx.enter_context(tc.tile_pool(name="keep", bufs=1))
+        arena = ctx.enter_context(tc.tile_pool(name="arena", bufs=1))
         ring = ctx.enter_context(tc.tile_pool(name="ring", bufs=2))
-        psum = ctx.enter_context(tc.psum_pool(name="psum", bufs=2))
+        psum = ctx.enter_context(tc.psum_pool(name="psum", bufs=1))
 
-        def held(name, shape, dtype, after=None):
-            return keep.tile(shape, dtype, name=name, tag=after or name, align_bytes=64)
+        def held(name, shape, dtype):
+            return keep.tile(shape, dtype, name=name, align_bytes=64)
+
+        def placed(name, shape, dtype, kib):
+            return arena.tile(shape, dtype, name=name, offset=kib * 1024, align_bytes=64)
+
+        def bank(number, shape):
+            return psum.tile(shape, F32, name="bank%d" % number)
 
         lookup_list = held("lookup_list", [P, S // 16], U16)
         put_list = held("put_list", [P, S // 16], U16)
@@ -77,21 +83,26 @@ def tile_list_sonobuoy_cue_features_kernel(
         w4_sc = held("w4_sc", [P, 1, N], U8)
         nc.gpsimd.memset(tab_sc[:].bitcast(I32), 0)
         nc.gpsimd.memset(w2_sc[:].bitcast(I32), 0)
+        zeros = placed("zeros", [P, 26 * 256], F32, 8)
         identity = held("identity", [P, P], F32)
-        make_identity(nc, identity[:])
-        load_scale_rows(nc.gpsimd, w2_sc, w2_scales)
+        nc.gpsimd.memset(zeros[:, :P], 0.0)
+        nc.gpsimd.affine_select(
+            out=identity[:], in_=zeros[:, :P], compare_op=ALU.not_equal, fill=1.0, base=0,
+            pattern=[[-1, P]], channel_multiplier=1,
+        )
         pages = [held("page%d" % i, [P, T2], F32) for i in range(PACK)]
         for page in pages:
-            nc.vector.memset(page[:], 0.0)
+            for half in range(2):
+                nc.gpsimd.memset(page[:, half * T2 // 2 : (half + 1) * T2 // 2], 0.0)
         for plane in (w5_sc, w4_sc):
             nc.gpsimd.memset(plane[:].bitcast(I32), 0)
 
         warm = held("warm", [P, 1], F32)
         nc.scalar.activation(warm[:], identity[:, 0:1], ACT.Sqrt, bias=1.0)
 
-        tab_w = [held("tab_w%d" % a, [P, T], I32) for a in range(PASSES)]
-        w1_raw = [held("w1_raw%d" % a, [P, PACK, H], F32) for a in range(PASSES)]
-        w2_w = held("w2_w", [P, PASSES, 2 * H], U8)
+        tab_w = [placed("tab_w%d" % a, [P, T], I32, 8 * a) for a in range(PASSES)]
+        w1_raw = [placed("w1_raw%d" % a, [P, PACK, H], F32, 16 + 8 * a) for a in range(PASSES)]
+        w2_w = placed("w2_w", [P, PASSES, 2 * H], U8, 32)
 
         def load_tab(a):
             nc.sync.dma_start(out=tab_w[a][:], in_=tab_words[a].rearrange("p t i -> p (t i)").bitcast(I32))
@@ -100,71 +111,58 @@ def tile_list_sonobuoy_cue_features_kernel(
             rows = w1[a * K_PASS : (a + 1) * K_PASS, :]
             nc.sync.dma_start(out=w1_raw[a][:], in_=rows.rearrange("(p i) r -> p i r", i=PACK))
 
-        load_scale_rows(nc.scalar, tab_sc, tab_scales)
         nc.sync.dma_start(lookup_list[:], offs)
         nc.sync.dma_start(put_list[:], offs2)
         nc.sync.dma_start(fetch_list[:], offs3)
-        load_w1(0)
         load_tab(0)
+        load_scale_rows(nc.sync, tab_sc, tab_scales)
+        load_scale_rows(nc.sync, w2_sc, w2_scales)
+        load_w1(0)
         load_w1(1)
         nc.sync.dma_start(out=w2_w[:].bitcast(I32), in_=w2_words.rearrange("a p c -> p a c").bitcast(I32))
         load_tab(1)
 
-        w1_codes = [held("w1_codes%d" % a, [P, H], U32) for a in range(PASSES)]
+        w1_codes = [placed("w1_codes%d" % a, [P, H], U32, 34 + 2 * a) for a in range(PASSES)]
         w1_sc = [held("w1_sc%d" % a, [P, H], U8) for a in range(PASSES)]
         w1_bf = [held("w1_bf%d" % a, [P, H, PACK], BF16) for a in range(PASSES)]
-        v_w = [[held("v_w%d_%d" % (a, lo), [P, hi - lo], U32) for lo, hi in spans(LOOKUP_CUTS)] for a in range(PASSES)]
-        v_sc = [[held("v_sc%d_%d" % (a, lo), [P, hi - lo], U8) for lo, hi in spans(LOOKUP_CUTS)] for a in range(PASSES)]
+        v_w = [placed("v_w%d" % a, [P, S], U32, 38 + 4 * a) for a in range(PASSES)]
+        v_sc = [held("v_sc%d" % a, [P, S], U8) for a in range(PASSES)]
 
         def looked_up(a, j0, width):
-            part = max(n for n, (lo, hi) in enumerate(spans(LOOKUP_CUTS)) if lo <= j0)
-            cols = slice(j0 - LOOKUP_CUTS[part], j0 - LOOKUP_CUTS[part] + width)
-            return v_w[a][part][:, cols].bitcast(FP8X4), v_sc[a][part][:, cols]
+            return v_w[a][:, j0 : j0 + width].bitcast(FP8X4), v_sc[a][:, j0 : j0 + width]
 
-        def look_up_words(a, part):
-            lo, hi = spans(LOOKUP_CUTS)[part]
-            nc.vector.tensor_copy(v_w[a][part][:], tab_w[a][:].bitcast(U32).indirect(entries(lookup_list, lo, hi)))
+        def look_up_words(a, lo, hi):
+            nc.vector.tensor_copy(v_w[a][:, lo:hi], tab_w[a][:].bitcast(U32).indirect(entries(lookup_list, lo, hi)))
 
-        def look_up_scales(part):
-            lo, hi = spans(LOOKUP_CUTS)[part]
-            for a in range(PASSES):
-                nc.vector.tensor_copy(v_sc[a][part][:], tab_sc[:, a, :].indirect(entries(lookup_list, lo, hi)))
-
+        look_up_words(0, 0, S)
+        for a in range(PASSES):
+            nc.vector.tensor_copy(v_sc[a][:], tab_sc[:, a, :].indirect(lookup_list[:]))
         for a in range(PASSES):
             interleave(nc, w1_bf[a][:], w1_raw[a][:])
-        look_up_scales(0)
-        look_up_scales(1)
-        quantize(nc, w1_codes[0][:], w1_sc[0][:], w1_bf[0][:])
-        for part in range(3):
-            look_up_words(0, part)
-        quantize(nc, w1_codes[1][:], w1_sc[1][:], w1_bf[1][:])
-        look_up_words(1, 0)
-        look_up_words(1, 1)
-        look_up_scales(2)
-        look_up_words(1, 2)
+            quantize(nc, w1_codes[a][:], w1_sc[a][:], w1_bf[a][:])
+        look_up_words(1, 0, FIRST_LOOKUP)
+        look_up_words(1, FIRST_LOOKUP, S)
 
-        wgs_sb = held("wgs_sb", [P, S], F32, after="w1_raw0")
-        w3_raw = held("w3_raw", [P, PACK, N], F32, after="w1_raw1")
-        w5_w = held("w5_w", [P, PASSES, N], I32, after="w1_bf0")
-        w4_w = held("w4_w", [P, 2 * N], U8, after="w1_bf1")
+        wgs_sb = placed("wgs_sb", [P, S], F32, 0)
+        w5_w = placed("w5_w", [P, PASSES, N], I32, 4)
+        w4_w = placed("w4_w", [P, 2 * N], U8, 6)
         nc.sync.dma_start(out=wgs_sb[:], in_=wgs)
         nc.sync.dma_start(out=w5_w[:], in_=w5_words.rearrange("a p c i -> p a (c i)").bitcast(I32))
-        nc.sync.dma_start(out=w3_raw[:], in_=w3.rearrange("(p i) n -> p i n", i=PACK))
         nc.sync.dma_start(out=w4_w[:].bitcast(I32), in_=w4_words[0].bitcast(I32))
         load_scale_rows(nc.sync, w5_sc, w5_scales)
         load_scale_rows(nc.sync, w4_sc, w4_scales)
         noise_rows = noise.rearrange("(p i) j -> p i j", i=PACK)
         noise_sb = []
         for a in range(PASSES):
-            pair = held("noise%d" % a, [P, 2, S], F32, after="tab_w%d" % a)
+            pair = placed("noise%d" % a, [P, 2, S], F32, 16 + 8 * a)
             nc.sync.dma_start(out=pair[:], in_=noise_rows[:, 2 * a : 2 * a + 2, :])
             noise_sb.extend([pair[:, 0, :], pair[:, 1, :]])
 
         for lo, hi in spans(PUT_CUTS):
             h = held("h%d" % lo, [P, PACK, hi - lo], F32)
             for j0 in range(lo, hi, P):
-                even = psum.tile([P, H], F32, name="even")
-                odd = psum.tile([P, H], F32, name="odd")
+                even = bank(j0 // P % 2, [P, H])
+                odd = bank(2 + j0 // P % 2, [P, H])
                 for a in range(PASSES):
                     nc.tensor.matmul_mx(
                         out=even[:], lhsT=looked_up(a, j0, P)[0], lhsT_scale=looked_up(a, j0, P)[1],
@@ -177,82 +175,138 @@ def tile_list_sonobuoy_cue_features_kernel(
                         rhs=w2_w[:, a, :].bitcast(FP4X4), rhs_scale=w2_sc[:, a, :],
                         start=(a == 0), stop=(a == PASSES - 1),
                     )
-                even_sq = ring.tile([P, PACK, P], F32, name="even_sq")
-                odd_sq = ring.tile([P, PACK, P], F32, name="odd_sq")
-                nc.scalar.activation(even_sq[:], even[:].rearrange("j (p i) -> j i p", i=PACK), ACT.Square)
-                nc.scalar.activation(odd_sq[:], odd[:].rearrange("j (p i) -> j i p", i=PACK), ACT.Square)
-                power = psum.tile([P, PACK, P], F32, name="power")
-                for i in range(PACK):
-                    nc.tensor.matmul(power[:, i, :], lhsT=even_sq[:, i, :], rhs=identity[:],
-                                     start=(i == 0), stop=False, is_transpose=True)
-                for i in range(PACK):
-                    nc.tensor.matmul(power[:, i, :], lhsT=odd_sq[:, i, :], rhs=identity[:],
-                                     start=False, stop=(i == PACK - 1), is_transpose=True)
-                nc.scalar.activation(h[:, :, j0 - lo : j0 - lo + P], power[:], ACT.Sqrt)
+                even_rows = even[:].rearrange("j (p i) -> j i p", i=PACK)
+                odd_rows = odd[:].rearrange("j (p i) -> j i p", i=PACK)
+                step = PACK // 2 if j0 == 0 else PACK
+                for i0 in range(0, PACK, step):
+                    even_sq = ring.tile([P, step, P], F32, name="even_sq")
+                    odd_sq = ring.tile([P, step, P], F32, name="odd_sq")
+                    nc.scalar.activation(even_sq[:], even_rows[:, i0 : i0 + step, :], ACT.Square)
+                    nc.scalar.activation(odd_sq[:], odd_rows[:, i0 : i0 + step, :], ACT.Square)
+                    power = bank(4 + (j0 // P + i0) % 4, [P, step, P])
+                    for i in range(step):
+                        nc.tensor.matmul(power[:, i, :], lhsT=even_sq[:, i, :], rhs=identity[:],
+                                         start=(i == 0), stop=False, is_transpose=True)
+                    for i in range(step):
+                        nc.tensor.matmul(power[:, i, :], lhsT=odd_sq[:, i, :], rhs=identity[:],
+                                         start=False, stop=(i == step - 1), is_transpose=True)
+                    nc.scalar.activation(h[:, i0 : i0 + step, j0 - lo : j0 - lo + P], power[:], ACT.Sqrt)
             for i in range(PACK):
                 nc.vector.tensor_tensor(
                     pages[i][:].indirect(entries(put_list, lo, hi)), h[:, i, :], wgs_sb[:, lo:hi], ALU.mult
                 )
 
-        skip_t = held("skip_t", [P, S // P, N], F32)
-        for pair in range(S // P // 2):
-            acc = psum.tile([P, 2, N], F32, name="power")
-            for u in range(2):
+        skip_t = held("skip_t", [P, TURNED // P, N], F32)
+        for j0 in range(0, TURNED, 2 * P):
+            blocks = min(2, (TURNED - j0) // P)
+            acc = bank(4 + j0 // (2 * P), [P, blocks, N])
+            for u in range(blocks):
                 for a in range(PASSES):
-                    codes, scales = looked_up(a, (2 * pair + u) * P, P)
+                    codes, scales = looked_up(a, j0 + u * P, P)
                     nc.tensor.matmul_mx(
                         out=acc[:, u, :], lhsT=codes, lhsT_scale=scales,
                         rhs=w5_w[:, a, :].bitcast(FP8X4), rhs_scale=w5_sc[:, a, :],
                         start=(a == 0), stop=(a == PASSES - 1),
                     )
-            nc.scalar.copy(out=skip_t[:, 2 * pair : 2 * pair + 2, :], in_=acc[:])
+            nc.scalar.copy(out=skip_t[:, j0 // P : j0 // P + blocks, :], in_=acc[:])
+        skip = held("skip", [P, N // P, S - TURNED], F32)
+        acc = bank(7, [P, N // P, S - TURNED])
+        for b in range(N // P):
+            rows = slice(b * P, (b + 1) * P)
+            for a in range(PASSES):
+                codes, scales = looked_up(a, TURNED, S - TURNED)
+                nc.tensor.matmul_mx(
+                    out=acc[:, b, :], lhsT=w5_w[:, a, rows].bitcast(FP8X4), lhsT_scale=w5_sc[:, a, rows],
+                    rhs=codes, rhs_scale=scales, start=(a == 0), stop=(a == PASSES - 1),
+                )
+        nc.scalar.copy(out=skip[:], in_=acc[:])
 
+        w3_raw = placed("w3_raw", [P, PACK, N], F32, 34)
+        nc.sync.dma_start(out=w3_raw[:], in_=w3.rearrange("(p i) n -> p i n", i=PACK))
         w3_codes = held("w3_codes", [P, N], U32)
         w3_sc = held("w3_sc", [P, N], U8)
-        w3_bf = held("w3_bf", [P, N, PACK], BF16)
+        w3_bf = placed("w3_bf", [P, N, PACK], BF16, 46)
         interleave(nc, w3_bf[:], w3_raw[:])
         quantize(nc, w3_codes[:], w3_sc[:], w3_bf[:])
 
         out_rows = out.rearrange("(b p) j -> p b j", p=P)
-        for lo, hi in spans(FETCH_CUTS):
+        chunks = spans(FETCH_CUTS)
+        y1_banks = (0, 1, 0, 6, 1)
+        y2_banks = (2, 3, 2, 6, 7)
+        total_banks = (4, 5, 0)
+
+        def project(chunk):
+            lo, hi = chunks[chunk]
             width = hi - lo
-            d = ring.tile([P, PACK, width], F32, name="d")
+            d = placed("d%d" % chunk, [P, PACK, width], F32, (38, 42, 8, 12, 38)[chunk])
             for i in range(PACK):
                 nc.vector.tensor_tensor(
                     d[:, i, :], pages[i][:].indirect(entries(fetch_list, lo, hi)), noise_sb[i][:, lo:hi], ALU.add
                 )
-            d_bf = ring.tile([P, width, PACK], BF16, name="d_bf", align_bytes=64)
+            d_bf = placed("d_bf%d" % chunk, [P, width, PACK], BF16, 46 + 2 * chunk)
             interleave(nc, d_bf[:], d[:])
-            d_codes = ring.tile([P, width], U32, name="d_codes", align_bytes=64)
-            d_sc = ring.tile([P, width], U8, name="d_sc", align_bytes=64)
+            d_codes = held("d_codes%d" % chunk, [P, width], U32)
+            d_sc = held("d_sc%d" % chunk, [P, width], U8)
             quantize(nc, d_codes[:], d_sc[:], d_bf[:])
-            blocks = width // P
-            y1 = psum.tile([P, blocks, N], F32, name="even")
-            y2 = psum.tile([P, blocks, N], F32, name="odd")
-            for u in range(blocks):
-                cols = slice(u * P, (u + 1) * P)
-                nc.tensor.matmul_mx(
-                    out=y1[:, u, :], lhsT=d_codes[:, cols].bitcast(FP8X4), lhsT_scale=d_sc[:, cols],
-                    rhs=w3_codes[:].bitcast(FP8X4), rhs_scale=w3_sc[:], start=True, stop=True,
-                )
-            for u in range(blocks):
-                cols = slice(u * P, (u + 1) * P)
-                nc.tensor.matmul_mx(
-                    out=y2[:, u, :], lhsT=d_codes[:, cols].bitcast(FP8X4), lhsT_scale=d_sc[:, cols],
-                    rhs=w4_w[:].bitcast(FP4X4), rhs_scale=w4_sc[:, 0, :], start=True, stop=True,
-                )
-            y1_sb = ring.tile([P, blocks, N], F32, name="y1_sb")
+            if lo < TURNED:
+                shape = [P, width // P, N]
+                y1, y2 = bank(y1_banks[chunk], shape), bank(y2_banks[chunk], shape)
+                for y, w_codes, w_sc in ((y1, w3_codes[:].bitcast(FP8X4), w3_sc[:]), (y2, w4_w[:].bitcast(FP4X4), w4_sc[:, 0, :])):
+                    for u in range(width // P):
+                        cols = slice(u * P, (u + 1) * P)
+                        nc.tensor.matmul_mx(
+                            out=y[:, u, :], lhsT=d_codes[:, cols].bitcast(FP8X4), lhsT_scale=d_sc[:, cols],
+                            rhs=w_codes, rhs_scale=w_sc, start=True, stop=True,
+                        )
+            else:
+                shape = [P, N // P, width]
+                if y1_banks[chunk] == y2_banks[chunk]:
+                    both = bank(y1_banks[chunk], [P, 2] + shape[1:])
+                    y1, y2 = both[:, 0], both[:, 1]
+                else:
+                    y1, y2 = bank(y1_banks[chunk], shape), bank(y2_banks[chunk], shape)
+                for b in range(N // P):
+                    rows = slice(b * P, (b + 1) * P)
+                    nc.tensor.matmul_mx(
+                        out=y1[:, b, :], lhsT=w3_codes[:, rows].bitcast(FP8X4), lhsT_scale=w3_sc[:, rows],
+                        rhs=d_codes[:].bitcast(FP8X4), rhs_scale=d_sc[:], start=True, stop=True,
+                    )
+                for b in range(N // P):
+                    rows = slice(b * P, (b + 1) * P)
+                    nc.tensor.matmul_mx(
+                        out=y2[:, b, :], lhsT=w4_w[:, 2 * b * P : 2 * (b + 1) * P].bitcast(FP4X4),
+                        lhsT_scale=w4_sc[:, 0, rows],
+                        rhs=d_codes[:].bitcast(FP8X4), rhs_scale=d_sc[:], start=True, stop=True,
+                    )
+            y1_sb = held("y1_sb%d" % chunk, shape, F32)
             nc.scalar.copy(out=y1_sb[:], in_=y1[:])
-            prod = ring.tile([P, blocks, N], F32, name="prod")
+            return shape, y1_sb, y2
+
+        def multiply(chunk, shape, y1_sb, y2):
+            prod = placed("prod%d" % chunk, shape, F32, 24 + 2 * (chunk - 1) if chunk else 4)
             nc.vector.tensor_tensor(prod[:], y2[:], y1_sb[:], ALU.mult)
-            total = psum.tile([P, N // P, width], F32, name="power")
-            squares = [(b, u) for u in range(blocks) for b in range(N // P)]
+            lo, hi = chunks[chunk]
+            if lo >= TURNED:
+                result = held("result%d" % chunk, shape, F32)
+                nc.vector.tensor_tensor(result[:], prod[:], skip[:, :, lo - TURNED : hi - TURNED], ALU.add)
+                nc.sync.dma_start(out=out_rows[:, :, lo:hi], in_=result[:])
+            return prod
+
+        projected = [project(0), project(1)]
+        prods = [multiply(0, *projected[0])]
+        projected.extend(project(chunk) for chunk in range(2, len(chunks)))
+        prods.extend(multiply(chunk, *projected[chunk]) for chunk in range(1, len(chunks)))
+
+        for chunk, (lo, hi) in enumerate(chunks[:3]):
+            width = hi - lo
+            total = bank(total_banks[chunk], [P, N // P, width])
+            squares = [(b, u) for u in range(width // P) for b in range(N // P)]
             for n, (b, u) in enumerate(squares):
                 nc.tensor.matmul(total[:, b, u * P : (u + 1) * P], lhsT=skip_t[:, lo // P + u, b * P : (b + 1) * P],
                                  rhs=identity[:], start=(n == 0), stop=False, is_transpose=True)
             for n, (b, u) in enumerate(squares):
-                nc.tensor.matmul(total[:, b, u * P : (u + 1) * P], lhsT=prod[:, u, b * P : (b + 1) * P],
+                nc.tensor.matmul(total[:, b, u * P : (u + 1) * P], lhsT=prods[chunk][:, u, b * P : (b + 1) * P],
                                  rhs=identity[:], start=False, stop=(n == len(squares) - 1), is_transpose=True)
-            result = ring.tile([P, N // P, width], F32, name="result")
+            result = held("result%d" % chunk, [P, N // P, width], F32)
             nc.scalar.copy(out=result[:], in_=total[:])
             nc.sync.dma_start(out=out_rows[:, :, lo:hi], in_=result[:])

from contextlib import ExitStack

import concourse.mybir as mybir

K, H, N, T, S, T2 = 1024, 512, 256, 2048, 1024, 2048
FLOPS = 2 * K * H * S * 2 + 2 * H * N * S * 2 + 2 * K * N * S

F32 = mybir.dt.float32
BF16 = mybir.dt.bfloat16
I32 = mybir.dt.int32
U32 = mybir.dt.uint32
U16 = mybir.dt.uint16
U8 = mybir.dt.uint8
FP8X4 = mybir.dt.float8_e4m3fn_x4
FP4X4 = mybir.dt.float4_e2m1fn_x4
ACT = mybir.ActivationFunctionType
ALU = mybir.AluOpType

P = 128
PACK = 4
K_PASS = P * PACK
PASSES = K // K_PASS
TURNED = 768
FIRST_LOOKUP = 256
PUT_CUTS = (0, 128, 256, 512, 768, 1024)
FETCH_CUTS = (0, 256, 512, 768, 896, 1024)


def spans(cuts):
    return list(zip(cuts[:-1], cuts[1:]))


def entries(offsets, lo, hi):
    return offsets[:, lo // 16 : hi // 16]


def load_scale_rows(queue, plane, scales):
    for q in range(4):
        queue.dma_start(
            out=plane[32 * q : 32 * q + 4].bitcast(I32),
            in_=scales[:, 4 * q : 4 * q + 4, :].rearrange("a r c -> r a c").bitcast(I32),
        )


def interleave(nc, grouped, rows):
    nc.scalar.copy(
        out=grouped.rearrange("p (c e) i -> p c i e", e=4),
        in_=rows.rearrange("p i (c e) -> p c i e", e=4),
    )


def quantize(nc, codes, scales, grouped):
    nc.vector.quantize_mx(out=codes.bitcast(FP8X4), scales=scales, in_=grouped.rearrange("p c i -> p (c i)"))


def tile_list_sonobuoy_cue_features_kernel(
    tc, tab_words, tab_scales, offs, offs2, offs3, w1, w2_words, w2_scales, wgs, noise, w3,
    w4_words, w4_scales, w5_words, w5_scales, out,
):
    nc = tc.nc
    with ExitStack() as ctx:
        keep = ctx.enter_context(tc.tile_pool(name="keep", bufs=1))
        arena = ctx.enter_context(tc.tile_pool(name="arena", bufs=1))
        ring = ctx.enter_context(tc.tile_pool(name="ring", bufs=2))
        psum = ctx.enter_context(tc.psum_pool(name="psum", bufs=1))

        def held(name, shape, dtype):
            return keep.tile(shape, dtype, name=name, align_bytes=64)

        def placed(name, shape, dtype, kib):
            return arena.tile(shape, dtype, name=name, offset=kib * 1024, align_bytes=64)

        def bank(number, shape):
            return psum.tile(shape, F32, name="bank%d" % number)

        lookup_list = held("lookup_list", [P, S // 16], U16)
        put_list = held("put_list", [P, S // 16], U16)
        fetch_list = held("fetch_list", [P, S // 16], U16)

        tab_sc = held("tab_sc", [P, PASSES, T], U8)
        w2_sc = held("w2_sc", [P, PASSES, H], U8)
        w5_sc = held("w5_sc", [P, PASSES, N], U8)
        w4_sc = held("w4_sc", [P, 1, N], U8)
        nc.gpsimd.memset(tab_sc[:].bitcast(I32), 0)
        nc.gpsimd.memset(w2_sc[:].bitcast(I32), 0)
        zeros = placed("zeros", [P, 26 * 256], F32, 8)
        identity = held("identity", [P, P], F32)
        nc.gpsimd.memset(zeros[:, :P], 0.0)
        nc.gpsimd.affine_select(
            out=identity[:], in_=zeros[:, :P], compare_op=ALU.not_equal, fill=1.0, base=0,
            pattern=[[-1, P]], channel_multiplier=1,
        )
        pages = [held("page%d" % i, [P, T2], F32) for i in range(PACK)]
        for page in pages:
            for half in range(2):
                nc.gpsimd.memset(page[:, half * T2 // 2 : (half + 1) * T2 // 2], 0.0)
        for plane in (w5_sc, w4_sc):
            nc.gpsimd.memset(plane[:].bitcast(I32), 0)

        warm = held("warm", [P, 1], F32)
        nc.scalar.activation(warm[:], identity[:, 0:1], ACT.Sqrt, bias=1.0)

        tab_w = [placed("tab_w%d" % a, [P, T], I32, 8 * a) for a in range(PASSES)]
        w1_raw = [placed("w1_raw%d" % a, [P, PACK, H], F32, 16 + 8 * a) for a in range(PASSES)]
        w2_w = placed("w2_w", [P, PASSES, 2 * H], U8, 32)

        def load_tab(a):
            nc.sync.dma_start(out=tab_w[a][:], in_=tab_words[a].rearrange("p t i -> p (t i)").bitcast(I32))

        def load_w1(a):
            rows = w1[a * K_PASS : (a + 1) * K_PASS, :]
            nc.sync.dma_start(out=w1_raw[a][:], in_=rows.rearrange("(p i) r -> p i r", i=PACK))

        nc.sync.dma_start(lookup_list[:], offs)
        nc.sync.dma_start(put_list[:], offs2)
        nc.sync.dma_start(fetch_list[:], offs3)
        load_tab(0)
        load_scale_rows(nc.sync, tab_sc, tab_scales)
        load_scale_rows(nc.sync, w2_sc, w2_scales)
        load_w1(0)
        load_w1(1)
        nc.sync.dma_start(out=w2_w[:].bitcast(I32), in_=w2_words.rearrange("a p c -> p a c").bitcast(I32))
        load_tab(1)

        w1_codes = [placed("w1_codes%d" % a, [P, H], U32, 34 + 2 * a) for a in range(PASSES)]
        w1_sc = [held("w1_sc%d" % a, [P, H], U8) for a in range(PASSES)]
        w1_bf = [held("w1_bf%d" % a, [P, H, PACK], BF16) for a in range(PASSES)]
        v_w = [placed("v_w%d" % a, [P, S], U32, 38 + 4 * a) for a in range(PASSES)]
        v_sc = [held("v_sc%d" % a, [P, S], U8) for a in range(PASSES)]

        def looked_up(a, j0, width):
            return v_w[a][:, j0 : j0 + width].bitcast(FP8X4), v_sc[a][:, j0 : j0 + width]

        def look_up_words(a, lo, hi):
            nc.vector.tensor_copy(v_w[a][:, lo:hi], tab_w[a][:].bitcast(U32).indirect(entries(lookup_list, lo, hi)))

        look_up_words(0, 0, S)
        for a in range(PASSES):
            nc.vector.tensor_copy(v_sc[a][:], tab_sc[:, a, :].indirect(lookup_list[:]))
        for a in range(PASSES):
            interleave(nc, w1_bf[a][:], w1_raw[a][:])
            quantize(nc, w1_codes[a][:], w1_sc[a][:], w1_bf[a][:])
        look_up_words(1, 0, FIRST_LOOKUP)
        look_up_words(1, FIRST_LOOKUP, S)

        wgs_sb = placed("wgs_sb", [P, S], F32, 0)
        w5_w = placed("w5_w", [P, PASSES, N], I32, 4)
        w4_w = placed("w4_w", [P, 2 * N], U8, 6)
        nc.sync.dma_start(out=wgs_sb[:], in_=wgs)
        nc.sync.dma_start(out=w5_w[:], in_=w5_words.rearrange("a p c i -> p a (c i)").bitcast(I32))
        nc.sync.dma_start(out=w4_w[:].bitcast(I32), in_=w4_words[0].bitcast(I32))
        load_scale_rows(nc.sync, w5_sc, w5_scales)
        load_scale_rows(nc.sync, w4_sc, w4_scales)
        noise_rows = noise.rearrange("(p i) j -> p i j", i=PACK)
        noise_sb = []
        for a in range(PASSES):
            pair = placed("noise%d" % a, [P, 2, S], F32, 16 + 8 * a)
            nc.sync.dma_start(out=pair[:], in_=noise_rows[:, 2 * a : 2 * a + 2, :])
            noise_sb.extend([pair[:, 0, :], pair[:, 1, :]])

        for lo, hi in spans(PUT_CUTS):
            h = held("h%d" % lo, [P, PACK, hi - lo], F32)
            for j0 in range(lo, hi, P):
                even = bank(j0 // P % 2, [P, H])
                odd = bank(2 + j0 // P % 2, [P, H])
                for a in range(PASSES):
                    nc.tensor.matmul_mx(
                        out=even[:], lhsT=looked_up(a, j0, P)[0], lhsT_scale=looked_up(a, j0, P)[1],
                        rhs=w1_codes[a][:].bitcast(FP8X4), rhs_scale=w1_sc[a][:],
                        start=(a == 0), stop=(a == PASSES - 1),
                    )
                for a in range(PASSES):
                    nc.tensor.matmul_mx(
                        out=odd[:], lhsT=looked_up(a, j0, P)[0], lhsT_scale=looked_up(a, j0, P)[1],
                        rhs=w2_w[:, a, :].bitcast(FP4X4), rhs_scale=w2_sc[:, a, :],
                        start=(a == 0), stop=(a == PASSES - 1),
                    )
                even_rows = even[:].rearrange("j (p i) -> j i p", i=PACK)
                odd_rows = odd[:].rearrange("j (p i) -> j i p", i=PACK)
                step = PACK // 2 if j0 == 0 else PACK
                for i0 in range(0, PACK, step):
                    even_sq = ring.tile([P, step, P], F32, name="even_sq")
                    odd_sq = ring.tile([P, step, P], F32, name="odd_sq")
                    nc.scalar.activation(even_sq[:], even_rows[:, i0 : i0 + step, :], ACT.Square)
                    nc.scalar.activation(odd_sq[:], odd_rows[:, i0 : i0 + step, :], ACT.Square)
                    power = bank(4 + (j0 // P + i0) % 4, [P, step, P])
                    for i in range(step):
                        nc.tensor.matmul(power[:, i, :], lhsT=even_sq[:, i, :], rhs=identity[:],
                                         start=(i == 0), stop=False, is_transpose=True)
                    for i in range(step):
                        nc.tensor.matmul(power[:, i, :], lhsT=odd_sq[:, i, :], rhs=identity[:],
                                         start=False, stop=(i == step - 1), is_transpose=True)
                    nc.scalar.activation(h[:, i0 : i0 + step, j0 - lo : j0 - lo + P], power[:], ACT.Sqrt)
            for i in range(PACK):
                nc.vector.tensor_tensor(
                    pages[i][:].indirect(entries(put_list, lo, hi)), h[:, i, :], wgs_sb[:, lo:hi], ALU.mult
                )

        skip_t = held("skip_t", [P, TURNED // P, N], F32)
        for j0 in range(0, TURNED, 2 * P):
            blocks = min(2, (TURNED - j0) // P)
            acc = bank(4 + j0 // (2 * P), [P, blocks, N])
            for u in range(blocks):
                for a in range(PASSES):
                    codes, scales = looked_up(a, j0 + u * P, P)
                    nc.tensor.matmul_mx(
                        out=acc[:, u, :], lhsT=codes, lhsT_scale=scales,
                        rhs=w5_w[:, a, :].bitcast(FP8X4), rhs_scale=w5_sc[:, a, :],
                        start=(a == 0), stop=(a == PASSES - 1),
                    )
            nc.scalar.copy(out=skip_t[:, j0 // P : j0 // P + blocks, :], in_=acc[:])
        skip = held("skip", [P, N // P, S - TURNED], F32)
        acc = bank(7, [P, N // P, S - TURNED])
        for b in range(N // P):
            rows = slice(b * P, (b + 1) * P)
            for a in range(PASSES):
                codes, scales = looked_up(a, TURNED, S - TURNED)
                nc.tensor.matmul_mx(
                    out=acc[:, b, :], lhsT=w5_w[:, a, rows].bitcast(FP8X4), lhsT_scale=w5_sc[:, a, rows],
                    rhs=codes, rhs_scale=scales, start=(a == 0), stop=(a == PASSES - 1),
                )
        nc.scalar.copy(out=skip[:], in_=acc[:])

        w3_raw = placed("w3_raw", [P, PACK, N], F32, 34)
        nc.sync.dma_start(out=w3_raw[:], in_=w3.rearrange("(p i) n -> p i n", i=PACK))
        w3_codes = held("w3_codes", [P, N], U32)
        w3_sc = held("w3_sc", [P, N], U8)
        w3_bf = placed("w3_bf", [P, N, PACK], BF16, 46)
        interleave(nc, w3_bf[:], w3_raw[:])
        quantize(nc, w3_codes[:], w3_sc[:], w3_bf[:])

        out_rows = out.rearrange("(b p) j -> p b j", p=P)
        chunks = spans(FETCH_CUTS)
        y1_banks = (0, 1, 0, 6, 1)
        y2_banks = (2, 3, 2, 6, 7)
        total_banks = (4, 5, 0)

        def project(chunk):
            lo, hi = chunks[chunk]
            width = hi - lo
            d = placed("d%d" % chunk, [P, PACK, width], F32, (38, 42, 8, 12, 38)[chunk])
            for i in range(PACK):
                nc.vector.tensor_tensor(
                    d[:, i, :], pages[i][:].indirect(entries(fetch_list, lo, hi)), noise_sb[i][:, lo:hi], ALU.add
                )
            d_bf = placed("d_bf%d" % chunk, [P, width, PACK], BF16, 46 + 2 * chunk)
            interleave(nc, d_bf[:], d[:])
            d_codes = held("d_codes%d" % chunk, [P, width], U32)
            d_sc = held("d_sc%d" % chunk, [P, width], U8)
            quantize(nc, d_codes[:], d_sc[:], d_bf[:])
            if lo < TURNED:
                shape = [P, width // P, N]
                y1, y2 = bank(y1_banks[chunk], shape), bank(y2_banks[chunk], shape)
                for y, w_codes, w_sc in ((y1, w3_codes[:].bitcast(FP8X4), w3_sc[:]), (y2, w4_w[:].bitcast(FP4X4), w4_sc[:, 0, :])):
                    for u in range(width // P):
                        cols = slice(u * P, (u + 1) * P)
                        nc.tensor.matmul_mx(
                            out=y[:, u, :], lhsT=d_codes[:, cols].bitcast(FP8X4), lhsT_scale=d_sc[:, cols],
                            rhs=w_codes, rhs_scale=w_sc, start=True, stop=True,
                        )
            else:
                shape = [P, N // P, width]
                if y1_banks[chunk] == y2_banks[chunk]:
                    both = bank(y1_banks[chunk], [P, 2] + shape[1:])
                    y1, y2 = both[:, 0], both[:, 1]
                else:
                    y1, y2 = bank(y1_banks[chunk], shape), bank(y2_banks[chunk], shape)
                for b in range(N // P):
                    rows = slice(b * P, (b + 1) * P)
                    nc.tensor.matmul_mx(
                        out=y1[:, b, :], lhsT=w3_codes[:, rows].bitcast(FP8X4), lhsT_scale=w3_sc[:, rows],
                        rhs=d_codes[:].bitcast(FP8X4), rhs_scale=d_sc[:], start=True, stop=True,
                    )
                for b in range(N // P):
                    rows = slice(b * P, (b + 1) * P)
                    nc.tensor.matmul_mx(
                        out=y2[:, b, :], lhsT=w4_w[:, 2 * b * P : 2 * (b + 1) * P].bitcast(FP4X4),
                        lhsT_scale=w4_sc[:, 0, rows],
                        rhs=d_codes[:].bitcast(FP8X4), rhs_scale=d_sc[:], start=True, stop=True,
                    )
            y1_sb = held("y1_sb%d" % chunk, shape, F32)
            nc.scalar.copy(out=y1_sb[:], in_=y1[:])
            return shape, y1_sb, y2

        def multiply(chunk, shape, y1_sb, y2):
            prod = placed("prod%d" % chunk, shape, F32, 24 + 2 * (chunk - 1) if chunk else 4)
            nc.vector.tensor_tensor(prod[:], y2[:], y1_sb[:], ALU.mult)
            lo, hi = chunks[chunk]
            if lo >= TURNED:
                result = held("result%d" % chunk, shape, F32)
                nc.vector.tensor_tensor(result[:], prod[:], skip[:, :, lo - TURNED : hi - TURNED], ALU.add)
                nc.sync.dma_start(out=out_rows[:, :, lo:hi], in_=result[:])
            return prod

        projected = [project(0), project(1)]
        prods = [multiply(0, *projected[0])]
        projected.extend(project(chunk) for chunk in range(2, len(chunks)))
        prods.extend(multiply(chunk, *projected[chunk]) for chunk in range(1, len(chunks)))

        for chunk, (lo, hi) in enumerate(chunks[:3]):
            width = hi - lo
            total = bank(total_banks[chunk], [P, N // P, width])
            squares = [(b, u) for u in range(width // P) for b in range(N // P)]
            for n, (b, u) in enumerate(squares):
                nc.tensor.matmul(total[:, b, u * P : (u + 1) * P], lhsT=skip_t[:, lo // P + u, b * P : (b + 1) * P],
                                 rhs=identity[:], start=(n == 0), stop=False, is_transpose=True)
            for n, (b, u) in enumerate(squares):
                nc.tensor.matmul(total[:, b, u * P : (u + 1) * P], lhsT=prods[chunk][:, u, b * P : (b + 1) * P],
                                 rhs=identity[:], start=False, stop=(n == len(squares) - 1), is_transpose=True)
            result = held("result%d" % chunk, [P, N // P, width], F32)
            nc.scalar.copy(out=result[:], in_=total[:])
            nc.sync.dma_start(out=out_rows[:, :, lo:hi], in_=result[:])
